import numpy as np
import ml_dtypes


def mxq(x, axis, fmt="e4m3"):
    dtype, down = {"e4m3": (ml_dtypes.float8_e4m3fn, 7), "e5m2": (ml_dtypes.float8_e5m2, 14)}[fmt]
    v = np.moveaxis(np.asarray(x, np.float32).astype(ml_dtypes.bfloat16).astype(np.float64), axis, -1)
    blocks = v.reshape(v.shape[:-1] + (-1, 32))
    amax = np.abs(blocks).max(-1, keepdims=True)
    byte = np.maximum(np.where(amax > 0, np.frexp(amax)[1] - 1 + 127, 0) - down, 1)
    scale = np.exp2(byte - 127.0)
    codes = (blocks / scale).astype(np.float32).astype(dtype).astype(np.float64)
    return np.moveaxis((codes * scale).reshape(v.shape), -1, axis)


WIDE = False


def mx_kscale(k):
    if not WIDE:
        return np.ones(k)
    levels = np.array([10, -10, 5, -5, 0])
    if k % 512:
        return np.exp2(np.random.permutation(np.resize(levels, k // 32))).repeat(32)
    a = np.empty((k // 512, 16))
    for p in range(k // 512):
        a[p, :8] = np.random.permutation(np.resize(levels, 8))
        for g in range(8):
            far = levels[np.abs(levels - a[p, g]) >= 10]
            a[p, g + 8] = far[np.random.randint(len(far))]
    return np.exp2(a.ravel()).repeat(32)


def f64(x):
    return np.asarray(x).astype(np.float64)


def striped(idx):
    return np.tile(idx.reshape(-1, 16).T, (8, 1)).astype(np.uint16)


def unstriped(offs):
    return offs[:16].T.reshape(-1).astype(np.int64)


def pack_weight(w):
    k, n = w.shape
    w = f64(np.asarray(w, np.float32).astype(ml_dtypes.bfloat16)).reshape(k // 32, 32, n)
    amax = np.abs(w).max(1)
    byte = np.clip(np.where(amax > 0, np.frexp(amax)[1] - 1 + 127 - 7, 1), 1, 254)
    scaled = (w * np.exp2(127.0 - byte)[:, None, :]).reshape(k, n).astype(np.float32)
    words = np.ascontiguousarray(scaled.reshape(k // 512, 128, 4, n).transpose(0, 1, 3, 2)).astype(ml_dtypes.float8_e4m3fn).view(np.uint8)
    return words, np.ascontiguousarray(byte.astype(np.uint8).reshape(k // 512, 16, n))


def unpack_weight(words, scales):
    g, p, n, _ = words.shape
    vals = np.ascontiguousarray(words).view(ml_dtypes.float8_e4m3fn).astype(np.float64) * np.repeat(np.exp2(scales.astype(np.float64) - 127.0), 8, axis=1)[..., None]
    return vals.transpose(0, 1, 3, 2).reshape(g * 512, n)


E2M1 = np.array([0.0, 0.5, 1.0, 1.5, 2.0, 3.0, 4.0, 6.0, -0.0, -0.5, -1.0, -1.5, -2.0, -3.0, -4.0, -6.0])


def pack_fp4(w):
    k, n = w.shape
    w = f64(np.asarray(w, np.float32).astype(ml_dtypes.bfloat16)).reshape(k // 32, 32, n)
    amax = np.abs(w).max(1)
    mant, ex = np.frexp(amax / 6.0)
    byte = np.clip(np.where(amax > 0, np.where(mant > 0.5, ex, ex - 1) + 127, 1), 1, 254)
    scaled = (w * np.exp2(127.0 - byte)[:, None, :]).reshape(k, n).astype(np.float32)
    c = np.ascontiguousarray(scaled.reshape(k // 512, 128, 4, n).transpose(0, 1, 3, 2)).astype(ml_dtypes.float4_e2m1fn).view(np.uint8) & 0xF
    words = (c[..., 0::2] | (c[..., 1::2] << 4)).reshape(k // 512, 128, 2 * n)
    return np.ascontiguousarray(words), np.ascontiguousarray(byte.astype(np.uint8).reshape(k // 512, 16, n))


def unpack_fp4(words, scales):
    g, _, n = scales.shape
    words = np.ascontiguousarray(words).reshape(g, 128, n, 2)
    nib = np.empty((g, 128, n, 4), np.uint8)
    nib[..., 0::2] = words & 0xF
    nib[..., 1::2] = words >> 4
    vals = E2M1[nib] * np.repeat(np.exp2(scales.astype(np.float64) - 127.0), 8, axis=1)[..., None]
    return vals.transpose(0, 1, 3, 2).reshape(g * 512, n)


def sigmoid(v):
    return 1.0 / (1.0 + np.exp(-np.maximum(v, -700.0)))


K, T, S, D, N, H, V, U = 512, 4096, 1024, 4, 128, 512, 256, 512


def setup_inputs():
    n = np.random.standard_normal
    s = mx_kscale(K)[:, None]
    u = mx_kscale(H)
    packed_xT = pack_weight(n((K, T)) * s)
    packed_w1 = pack_fp4(n((K, H)) / np.sqrt(K) / s)
    packed_w2 = pack_fp4(n((K, H)) / np.sqrt(K) / s)
    packed_w3 = pack_fp4(n((H, N)) / np.sqrt(H) / u[:, None])
    return {
        "x_words": packed_xT[0],
        "x_scales": packed_xT[1],
        "w1_words": packed_w1[0],
        "w1_scales": packed_w1[1],
        "w2_words": packed_w2[0],
        "w2_scales": packed_w2[1],
        "qa": (n((H, U))).astype(np.float32),
        "qb": (n((H, U))).astype(np.float32),
        "unit": (np.random.uniform(0.6, 1.4, (H, 1)) * u[:, None]).astype(np.float32),
        "w3_words": packed_w3[0],
        "w3_scales": packed_w3[1],
        "offs": striped(np.random.permutation(T)[:S]),
        "doc": striped(np.random.permutation(np.concatenate([np.arange(V), np.random.randint(0, V, U - V)]))),
        "alt": striped(np.random.permutation(np.concatenate([np.arange(V), np.random.randint(0, V, U - V)]))),
    }


def reference(x_words, x_scales, w1_words, w1_scales, w2_words, w2_scales, qa, qb, unit, w3_words, w3_scales, offs, doc, alt):
    xq = unpack_weight(x_words, x_scales)[:, unstriped(offs)]
    y = unpack_fp4(w1_words, w1_scales).T @ xq
    yb = unpack_fp4(w2_words, w2_scales).T @ xq
    side = sigmoid(2.0 * yb)
    ya = y * side
    fa = ya.reshape(len(ya), -1, D).sum(axis=2)
    ga = fa[:, unstriped(doc)]
    yo = y * (-1.0 * side + 1.0)
    fb = yo.reshape(len(yo), -1, D).sum(axis=2)
    gb = fb[:, unstriped(alt)]
    z = ga * f64(qa) + gb * f64(qb)
    hid = f64(unit) * (z / (np.abs(fa[:, unstriped(doc)]) + np.abs(fb[:, unstriped(alt)]) + 1.0))
    return unpack_fp4(w3_words, w3_scales).T @ mxq(hid, 0, "e4m3")

@@ -1,0 +1,238 @@
+from contextlib import ExitStack
+
+import concourse.mybir as mybir
+from concourse.masks import make_identity
+
+K, T, S, D, N, H, V, U = 512, 4096, 1024, 4, 128, 512, 256, 512
+FLOPS = 2 * K * H * S * 2 + 2 * H * N * U
+
+F32 = mybir.dt.float32
+BF16 = mybir.dt.bfloat16
+I32 = mybir.dt.int32
+U32 = mybir.dt.uint32
+U16 = mybir.dt.uint16
+U8 = mybir.dt.uint8
+FP8X4 = mybir.dt.float8_e4m3fn_x4
+FP4X4 = mybir.dt.float4_e2m1fn_x4
+ACT = mybir.ActivationFunctionType
+ALU = mybir.AluOpType
+
+P = 128
+SLOTS = 4
+HALF = U // 2
+WINDOW = 768
+
+
+def tile_picked_ymuver_rel_p_kernel(
+    tc, x_words, x_scales, w1_words, w1_scales, w2_words, w2_scales, qa, qb, unit, w3_words, w3_scales,
+    offs, doc, alt, out,
+):
+    nc = tc.nc
+    with ExitStack() as ctx:
+        keep = ctx.enter_context(tc.tile_pool(name="keep", bufs=1))
+        work = ctx.enter_context(tc.tile_pool(name="work", bufs=2))
+        psum = ctx.enter_context(tc.psum_pool(name="psum", bufs=1))
+
+        offs_t = keep.tile([P, S // 16], U16, name="offs_t")
+        doc_t = keep.tile([P, U // 16], U16, name="doc_t")
+        alt_t = keep.tile([P, U // 16], U16, name="alt_t")
+        nc.sync.dma_start(offs_t[:], offs)
+        nc.sync.dma_start(doc_t[:], doc)
+        nc.sync.dma_start(alt_t[:], alt)
+
+        w_raw = []
+        for j, words in enumerate((w1_words, w2_words)):
+            raw = keep.tile([P, 2 * H], U8, name="w_raw%d" % j, tag="wq%d" % j, align_bytes=64)
+            nc.sync.dma_start(raw[:].bitcast(I32), words[0].bitcast(I32))
+            w_raw.append(raw)
+        xw = keep.tile([P, T], U32, name="xw")
+        nc.sync.dma_start(xw[:].bitcast(I32), x_words[0].rearrange("p n t -> p (n t)").bitcast(I32))
+
+        xs = keep.tile([P, T], U8, name="xs")
+        nc.vector.memset(xs[:].bitcast(I32), 0)
+        ws_raw = [keep.tile([P, H], U8, name="ws_raw%d" % j, tag="late%d" % j, align_bytes=64) for j in range(2)]
+        nc.vector.memset(ws_raw[0][:].bitcast(I32), 0)
+        nc.gpsimd.memset(ws_raw[1][:].bitcast(I32), 0)
+
+        def load_scale_rows(queue, plane, scales, q):
+            queue.dma_start(plane[32 * q : 32 * q + 4, :].bitcast(I32), scales[0, 4 * q : 4 * q + 4, :].bitcast(I32))
+
+        for q in range(4):
+            load_scale_rows(nc.scalar, xs, x_scales, q)
+        for q in range(4):
+            load_scale_rows(nc.gpsimd, ws_raw[1], w2_scales, q)
+        for q in range(4):
+            load_scale_rows(nc.scalar if q < 3 else nc.gpsimd, ws_raw[0], w1_scales, q)
+
+        ident = keep.tile([P, P], F32, name="ident")
+        make_identity(nc, ident[:])
+        one = keep.tile([P, 1], F32, name="one")
+        nc.gpsimd.memset(one[:], 1.0)
+        tables = []
+        for t in range(SLOTS):
+            table = keep.tile([P, 4 * V], F32, name="table%d" % t)
+            nc.gpsimd.memset(table[:, 2 * V :], 0.0)
+            tables.append(table)
+
+        w_dealt = []
+        for j in range(2):
+            dealt = keep.tile([P, SLOTS, P, 2], U8, name="w_dealt%d" % j, align_bytes=64)
+            nc.vector.tensor_copy(dealt[:], w_raw[j][:].rearrange("p (m t b) -> p t m b", t=SLOTS, b=2))
+            w_dealt.append(dealt)
+
+        gs_dealt = [keep.tile([P, D, P], U8, name="gs_dealt%d" % h, align_bytes=64) for h in range(2)]
+
+        def gather_scales(h):
+            gs = keep.tile([P, S // 2], U8, name="gs%d" % h, tag="late%d" % (2 + h), align_bytes=64)
+            nc.vector.tensor_copy(gs[:], xs[:].indirect(offs_t[:, 32 * h : 32 * (h + 1)]))
+            nc.vector.tensor_copy(gs_dealt[h][:], gs[:].rearrange("p (v d) -> p d v", d=D))
+
+        gather_scales(0)
+        ws_dealt = [keep.tile([P, SLOTS, P], U8, name="ws_dealt%d" % j, align_bytes=64) for j in range(2)]
+        for j in range(2):
+            nc.vector.tensor_copy(ws_dealt[j][:], ws_raw[j][:].rearrange("p (m t) -> p t m", t=SLOTS))
+        gather_scales(1)
+
+        q_t = [keep.tile([P, SLOTS, U], F32, name="q%d" % j, tag="late%d" % j, align_bytes=64) for j in range(2)]
+        for pair in range(2):
+            for j, q_in in enumerate((qa, qb)):
+                rows = slice(2 * pair, 2 * pair + 2)
+                nc.sync.dma_start(q_t[j][:, rows, :], q_in.rearrange("(p t) r -> p t r", t=SLOTS)[:, rows, :])
+        unit_t = keep.tile([P, SLOTS], F32, name="unit_t", tag="wq0", align_bytes=64)
+        nc.sync.dma_start(unit_t[:], unit.rearrange("(p t) o -> p (t o)", t=SLOTS))
+        w3w = keep.tile([P, 2 * N], U8, name="w3w", tag="wq1", align_bytes=64)
+        nc.sync.dma_start(w3w[:].bitcast(I32), w3_words[0].bitcast(I32))
+        w3s = keep.tile([P, N], U8, name="w3s", tag="late3", align_bytes=64)
+        nc.gpsimd.memset(w3s[:].bitcast(I32), 0)
+        for q in range(4):
+            load_scale_rows(nc.sync, w3s, w3_scales, q)
+
+        neg_unit = keep.tile([P, SLOTS], F32, name="neg_unit")
+        nc.vector.tensor_scalar(neg_unit[:], unit_t[:], -1.0, None, ALU.mult)
+
+        gw = [keep.tile([P, D, P], U32, name="gw%d" % h, align_bytes=64) for h in range(2)]
+
+        def gather_words(h):
+            nc.vector.tensor_copy(gw[h][:].rearrange("p d v -> p v d"), xw[:].indirect(offs_t[:, 32 * h : 32 * (h + 1)]))
+
+        def products(bank, j, t, h):
+            for d in range(D):
+                nc.tensor.matmul_mx(
+                    out=bank[:, d, :],
+                    lhsT=gw[h][:, d, :].bitcast(FP8X4),
+                    lhsT_scale=gs_dealt[h][:, d, :],
+                    rhs=w_dealt[j][:, t].rearrange("p m b -> p (m b)").bitcast(FP4X4),
+                    rhs_scale=ws_dealt[j][:, t, :],
+                    start=True,
+                    stop=True,
+                )
+
+        def sum_turned(target, parts):
+            blocks = [part[:, d, :] for part in parts for d in range(D)]
+            for n, block in enumerate(blocks):
+                nc.tensor.matmul(target, lhsT=block, rhs=ident[:], is_transpose=True, start=(n == 0), stop=(n == len(blocks) - 1))
+
+        def encode_half(t, h, acc):
+            y_bank = psum.tile([P, D, P], F32, name="y_bank", bufs=3)
+            yb_bank = psum.tile([P, D, P], F32, name="yb_bank", bufs=2)
+            products(y_bank, 0, t, h)
+            products(yb_bank, 1, t, h)
+            y_neg2 = work.tile([P, D, P], F32, name="y_neg2")
+            nc.scalar.activation(y_neg2[:], y_bank[:], ACT.Copy, scale=-2.0)
+            last = t == SLOTS - 1 and h == 1
+            pool = keep if last else work
+            th = pool.tile([P, D, P], F32, name="th", tag="last_tanh" if last else "th")
+            nc.scalar.activation(th[:], yb_bank[:], ACT.Tanh)
+            ya2 = work.tile([P, D, P], F32, name="ya2")
+            nc.vector.scalar_tensor_tensor(
+                ya2[:].rearrange("p d m -> p (d m)"), th[:].rearrange("p d m -> p (d m)"), 1.0,
+                y_bank[:].rearrange("p d m -> p (d m)"), ALU.add, ALU.mult,
+            )
+            sum_turned(acc[:, h * P : (h + 1) * P], [ya2])
+            sum_turned(acc[:, V + h * P : V + (h + 1) * P], [y_neg2, ya2])
+
+        def encode(t):
+            acc = psum.tile([P, 2 * V], F32, name="acc", bufs=2)
+            for h in range(2):
+                if t == 0:
+                    gather_words(h)
+                encode_half(t, h, acc)
+            nc.scalar.activation(tables[t][:, : 2 * V], acc[:], ACT.Copy, scale=0.5)
+
+        z = keep.tile([P, 2, SLOTS, HALF], F32, name="z")
+        inv = keep.tile([P, 2, SLOTS, HALF], F32, name="inv")
+        dens = {}
+
+        def look_up(t, halves):
+            r0, width = halves[0] * HALF, len(halves) * HALF
+            cols = slice(r0 // 16, (r0 + width) // 16)
+            g = work.tile([P, 2, width], F32, name="g")
+            nc.vector.tensor_copy(g[:, 0, :], tables[t][:, 0:WINDOW].indirect(doc_t[:, cols]))
+            nc.vector.tensor_copy(g[:, 1, :], tables[t][:, V : V + WINDOW].indirect(alt_t[:, cols]))
+            mag = work.tile([P, 2, width], F32, name="mag")
+            for j in range(2):
+                nc.scalar.activation(mag[:, j, :], g[:, j, :], ACT.Abs)
+            prod = work.tile([P, 2, width], F32, name="prod")
+            for j, factor in enumerate((unit_t, neg_unit)):
+                nc.vector.scalar_tensor_tensor(
+                    prod[:, j, :], g[:, j, :], factor[:, t : t + 1], q_t[j][:, t, r0 : r0 + width], ALU.mult, ALU.mult
+                )
+            den = keep.tile([P, width], F32, name="den%d_%d" % (t, halves[0]))
+            nc.vector.tensor_tensor(den[:], mag[:, 0, :], mag[:, 1, :], ALU.add)
+            dens[(t, halves[0])] = den
+            nc.vector.tensor_tensor(
+                z[:, halves[0] : halves[-1] + 1, t, :],
+                prod[:, 0, :].rearrange("p (h r) -> p h r", r=HALF),
+                prod[:, 1, :].rearrange("p (h r) -> p h r", r=HALF),
+                ALU.add,
+            )
+
+        def invert(t, halves):
+            width = len(halves) * HALF
+            first = t == 0
+            pool = keep if first else work
+            root = pool.tile([P, width], F32, name="root", tag="last_tanh" if first else "root")
+            nc.scalar.activation(root[:], dens[(t, halves[0])][:], ACT.Abs_reciprocal_sqrt, bias=one[:])
+            nc.scalar.activation(
+                inv[:, halves[0] : halves[-1] + 1, t, :], root[:].rearrange("p (h r) -> p h r", r=HALF), ACT.Square
+            )
+
+        out_bank = psum.tile([P, U], F32, name="out_bank")
+
+        def project(h):
+            hid = work.tile([P, HALF, SLOTS], BF16, name="hid", align_bytes=64)
+            nc.vector.tensor_tensor(
+                hid[:].rearrange("p (c i) t -> p c t i", i=4),
+                z[:, h].rearrange("p t (c i) -> p c t i", i=4),
+                inv[:, h].rearrange("p t (c i) -> p c t i", i=4),
+                ALU.mult,
+            )
+            codes = work.tile([P, HALF], U32, name="codes", align_bytes=64)
+            scales = work.tile([P, HALF], U8, name="scales", align_bytes=64)
+            nc.vector.quantize_mx(out=codes[:].bitcast(FP8X4), scales=scales[:], in_=hid[:].rearrange("p r t -> p (r t)"))
+            cols = slice(h * HALF, (h + 1) * HALF)
+            nc.tensor.matmul_mx(
+                out=out_bank[:, cols], lhsT=w3w[:].bitcast(FP4X4), lhsT_scale=w3s[:],
+                rhs=codes[:].bitcast(FP8X4), rhs_scale=scales[:], start=True, stop=True,
+            )
+            result = work.tile([P, HALF], F32, name="result")
+            nc.scalar.copy(result[:], out_bank[:, cols])
+            nc.sync.dma_start(out[:, cols], result[:])
+
+        both = (0, 1)
+        encode(0)
+        encode(1)
+        look_up(0, both)
+        encode(2)
+        look_up(1, both)
+        encode(3)
+        invert(0, both)
+        look_up(2, both)
+        invert(1, both)
+        look_up(3, (0,))
+        invert(2, both)
+        invert(3, (0,))
+        look_up(3, (1,))
+        project(0)
+        invert(3, (1,))
+        project(1)

@@ -42,7 +42,7 @@ def tile_picked_ymuver_rel_p_kernel(
 
         w_raw = []
         for j, words in enumerate((w1_words, w2_words)):
-            raw = keep.tile([P, 2 * H], U8, name="w_raw%d" % j, tag="wq%d" % j, align_bytes=64)
+            raw = keep.tile([P, 2 * H], U8, name="w_raw%d" % j, align_bytes=64)
             nc.sync.dma_start(raw[:].bitcast(I32), words[0].bitcast(I32))
             w_raw.append(raw)
         xw = keep.tile([P, T], U32, name="xw")
@@ -66,8 +66,8 @@ def tile_picked_ymuver_rel_p_kernel(
 
         ident = keep.tile([P, P], F32, name="ident")
         make_identity(nc, ident[:])
-        one = keep.tile([P, 1], F32, name="one")
-        nc.gpsimd.memset(one[:], 1.0)
+        two = keep.tile([P, 1], F32, name="two")
+        nc.gpsimd.memset(two[:], 2.0)
         tables = []
         for t in range(SLOTS):
             table = keep.tile([P, 4 * V], F32, name="table%d" % t)
@@ -91,24 +91,19 @@ def tile_picked_ymuver_rel_p_kernel(
         ws_dealt = [keep.tile([P, SLOTS, P], U8, name="ws_dealt%d" % j, align_bytes=64) for j in range(2)]
         for j in range(2):
             nc.vector.tensor_copy(ws_dealt[j][:], ws_raw[j][:].rearrange("p (m t) -> p t m", t=SLOTS))
-        gather_scales(1)
 
-        q_t = [keep.tile([P, SLOTS, U], F32, name="q%d" % j, tag="late%d" % j, align_bytes=64) for j in range(2)]
+        q_flat = [keep.tile([P, SLOTS * U + SLOTS], F32, name="q%d" % j, tag="late%d" % j, align_bytes=64) for j in range(2)]
+        q_t = [flat[:, : SLOTS * U].rearrange("p (t r) -> p t r", t=SLOTS) for flat in q_flat]
+        unit_t = q_flat[0][:, SLOTS * U :]
+        neg_unit = q_flat[1][:, SLOTS * U :]
+        nc.sync.dma_start(unit_t, unit.rearrange("(p t) o -> p (t o)", t=SLOTS))
         for pair in range(2):
             for j, q_in in enumerate((qa, qb)):
                 rows = slice(2 * pair, 2 * pair + 2)
                 nc.sync.dma_start(q_t[j][:, rows, :], q_in.rearrange("(p t) r -> p t r", t=SLOTS)[:, rows, :])
-        unit_t = keep.tile([P, SLOTS], F32, name="unit_t", tag="wq0", align_bytes=64)
-        nc.sync.dma_start(unit_t[:], unit.rearrange("(p t) o -> p (t o)", t=SLOTS))
-        w3w = keep.tile([P, 2 * N], U8, name="w3w", tag="wq1", align_bytes=64)
+        w3w = keep.tile([P, 2 * N], U8, name="w3w", tag="late2", align_bytes=64)
         nc.sync.dma_start(w3w[:].bitcast(I32), w3_words[0].bitcast(I32))
-        w3s = keep.tile([P, N], U8, name="w3s", tag="late3", align_bytes=64)
-        nc.gpsimd.memset(w3s[:].bitcast(I32), 0)
-        for q in range(4):
-            load_scale_rows(nc.sync, w3s, w3_scales, q)
-
-        neg_unit = keep.tile([P, SLOTS], F32, name="neg_unit")
-        nc.vector.tensor_scalar(neg_unit[:], unit_t[:], -1.0, None, ALU.mult)
+        nc.vector.tensor_scalar(neg_unit, unit_t, -1.0, None, ALU.mult)
 
         gw = [keep.tile([P, D, P], U32, name="gw%d" % h, align_bytes=64) for h in range(2)]
 
@@ -121,43 +116,82 @@ def tile_picked_ymuver_rel_p_kernel(
                     out=bank[:, d, :],
                     lhsT=gw[h][:, d, :].bitcast(FP8X4),
                     lhsT_scale=gs_dealt[h][:, d, :],
-                    rhs=w_dealt[j][:, t].rearrange("p m b -> p (m b)").bitcast(FP4X4),
+                    rhs=weights(j, t),
                     rhs_scale=ws_dealt[j][:, t, :],
                     start=True,
                     stop=True,
                 )
 
-        def sum_turned(target, parts):
-            blocks = [part[:, d, :] for part in parts for d in range(D)]
-            for n, block in enumerate(blocks):
-                nc.tensor.matmul(target, lhsT=block, rhs=ident[:], is_transpose=True, start=(n == 0), stop=(n == len(blocks) - 1))
+        def flat(tile):
+            return tile[:].rearrange("p a b -> p (a b)")
 
-        def encode_half(t, h, acc):
-            y_bank = psum.tile([P, D, P], F32, name="y_bank", bufs=3)
-            yb_bank = psum.tile([P, D, P], F32, name="yb_bank", bufs=2)
-            products(y_bank, 0, t, h)
-            products(yb_bank, 1, t, h)
-            y_neg2 = work.tile([P, D, P], F32, name="y_neg2")
-            nc.scalar.activation(y_neg2[:], y_bank[:], ACT.Copy, scale=-2.0)
-            last = t == SLOTS - 1 and h == 1
+        def weights(j, t):
+            return w_dealt[j][:, t].rearrange("p m b -> p (m b)").bitcast(FP4X4)
+
+        def sum_turned(target, part):
+            for d in range(D):
+                nc.tensor.matmul(target, lhsT=part[:, d, :], rhs=ident[:], is_transpose=True, start=(d == 0), stop=(d == D - 1))
+
+        def sum_of_products(target, t, h):
+            for d in range(D):
+                nc.tensor.matmul_mx(
+                    out=target, lhsT=weights(0, t), lhsT_scale=ws_dealt[0][:, t, :],
+                    rhs=gw[h][:, d, :].bitcast(FP8X4), rhs_scale=gs_dealt[h][:, d, :], start=(d == 0), stop=(d == D - 1),
+                )
+
+        def gate(y_bank, yb_bank, last):
             pool = keep if last else work
             th = pool.tile([P, D, P], F32, name="th", tag="last_tanh" if last else "th")
             nc.scalar.activation(th[:], yb_bank[:], ACT.Tanh)
-            ya2 = work.tile([P, D, P], F32, name="ya2")
-            nc.vector.scalar_tensor_tensor(
-                ya2[:].rearrange("p d m -> p (d m)"), th[:].rearrange("p d m -> p (d m)"), 1.0,
-                y_bank[:].rearrange("p d m -> p (d m)"), ALU.add, ALU.mult,
+            ya2 = work.tile([P, D, P], F32, name="ya2", bufs=3)
+            nc.vector.scalar_tensor_tensor(flat(ya2), flat(th), 1.0, flat(y_bank), ALU.add, ALU.mult)
+            return ya2
+
+        def banks():
+            return psum.tile([P, D, P], F32, name="y_bank", bufs=3), psum.tile([P, D, P], F32, name="yb_bank", bufs=2)
+
+        def other_side(t, acc):
+            nc.vector.scalar_tensor_tensor(tables[t][:, V : 2 * V], acc[:, V:], -2.0, tables[t][:, :V], ALU.mult, ALU.add)
+
+        def encode_first():
+            acc = psum.tile([P, 2 * V], F32, name="acc", bufs=2)
+            pairs = keep.tile([P, 2, 2, P], F32, name="pairs")
+            for h in range(2):
+                if h == 1:
+                    gather_scales(h)
+                gather_words(h)
+                y_bank, yb_bank = banks()
+                for j, bank in ((1, yb_bank), (0, y_bank)):
+                    nc.tensor.matmul_mx(
+                        out=flat(bank), lhsT=weights(j, 0), lhsT_scale=ws_dealt[j][:, 0, :],
+                        rhs=flat(gw[h]).bitcast(FP8X4), rhs_scale=flat(gs_dealt[h]), start=True, stop=True,
+                    )
+                sum_of_products(acc[:, V + h * P : V + (h + 1) * P], 0, h)
+                ya2 = gate(y_bank, yb_bank, False)
+                nc.vector.tensor_tensor(pairs[:, h], ya2[:, 0:2, :], ya2[:, 2:4, :], ALU.add)
+            nc.vector.tensor_tensor(
+                tables[0][:, :V].rearrange("p (h v) -> p h v", h=2), pairs[:, :, 0, :], pairs[:, :, 1, :], ALU.add
             )
-            sum_turned(acc[:, h * P : (h + 1) * P], [ya2])
-            sum_turned(acc[:, V + h * P : V + (h + 1) * P], [y_neg2, ya2])
+            other_side(0, acc)
 
         def encode(t):
             acc = psum.tile([P, 2 * V], F32, name="acc", bufs=2)
             for h in range(2):
-                if t == 0:
-                    gather_words(h)
-                encode_half(t, h, acc)
-            nc.scalar.activation(tables[t][:, : 2 * V], acc[:], ACT.Copy, scale=0.5)
+                y_bank, yb_bank = banks()
+                products(y_bank, 0, t, h)
+                products(yb_bank, 1, t, h)
+                y_sum = acc[:, V + h * P : V + (h + 1) * P]
+                if t == 1:
+                    sum_of_products(y_sum, t, h)
+                else:
+                    y_copy = work.tile([P, D, P], F32, name="y_copy")
+                    nc.scalar.copy(y_copy[:], y_bank[:])
+                ya2 = gate(y_bank, yb_bank, t == SLOTS - 1 and h == 1)
+                if t != 1:
+                    sum_turned(y_sum, y_copy)
+                sum_turned(acc[:, h * P : (h + 1) * P], ya2)
+            nc.scalar.copy(tables[t][:, :V], acc[:, :V])
+            other_side(t, acc)
 
         z = keep.tile([P, 2, SLOTS, HALF], F32, name="z")
         inv = keep.tile([P, 2, SLOTS, HALF], F32, name="inv")
@@ -172,14 +206,14 @@ def tile_picked_ymuver_rel_p_kernel(
             mag = work.tile([P, 2, width], F32, name="mag")
             for j in range(2):
                 nc.scalar.activation(mag[:, j, :], g[:, j, :], ACT.Abs)
+            den = keep.tile([P, width], F32, name="den%d_%d" % (t, halves[0]))
+            nc.vector.tensor_tensor(den[:], mag[:, 0, :], mag[:, 1, :], ALU.add)
+            dens[(t, halves[0])] = den
             prod = work.tile([P, 2, width], F32, name="prod")
             for j, factor in enumerate((unit_t, neg_unit)):
                 nc.vector.scalar_tensor_tensor(
                     prod[:, j, :], g[:, j, :], factor[:, t : t + 1], q_t[j][:, t, r0 : r0 + width], ALU.mult, ALU.mult
                 )
-            den = keep.tile([P, width], F32, name="den%d_%d" % (t, halves[0]))
-            nc.vector.tensor_tensor(den[:], mag[:, 0, :], mag[:, 1, :], ALU.add)
-            dens[(t, halves[0])] = den
             nc.vector.tensor_tensor(
                 z[:, halves[0] : halves[-1] + 1, t, :],
                 prod[:, 0, :].rearrange("p (h r) -> p h r", r=HALF),
@@ -192,7 +226,7 @@ def tile_picked_ymuver_rel_p_kernel(
             first = t == 0
             pool = keep if first else work
             root = pool.tile([P, width], F32, name="root", tag="last_tanh" if first else "root")
-            nc.scalar.activation(root[:], dens[(t, halves[0])][:], ACT.Abs_reciprocal_sqrt, bias=one[:])
+            nc.scalar.activation(root[:], dens[(t, halves[0])][:], ACT.Abs_reciprocal_sqrt, bias=two[:])
             nc.scalar.activation(
                 inv[:, halves[0] : halves[-1] + 1, t, :], root[:].rearrange("p (h r) -> p h r", r=HALF), ACT.Square
             )
@@ -220,12 +254,15 @@ def tile_picked_ymuver_rel_p_kernel(
             nc.sync.dma_start(out[:, cols], result[:])
 
         both = (0, 1)
-        encode(0)
-        encode(1)
+        encode_first()
+        w3s = keep.tile([P, N], U8, name="w3s", tag="late3", align_bytes=64)
+        nc.gpsimd.memset(w3s[:].bitcast(I32), 0)
+        for q in range(4):
+            load_scale_rows(nc.sync, w3s, w3_scales, q)
+        for t in range(1, SLOTS):
+            encode(t)
         look_up(0, both)
-        encode(2)
         look_up(1, both)
-        encode(3)
         invert(0, both)
         look_up(2, both)
         invert(1, both)
@@ -233,6 +270,6 @@ def tile_picked_ymuver_rel_p_kernel(
         invert(2, both)
         invert(3, (0,))
         look_up(3, (1,))
-        project(0)
         invert(3, (1,))
+        project(0)
         project(1)

@@ -40,32 +40,34 @@ def tile_picked_ymuver_rel_p_kernel(
         nc.sync.dma_start(doc_t[:], doc)
         nc.sync.dma_start(alt_t[:], alt)
 
-        w_raw = []
-        for j, words in enumerate((w1_words, w2_words)):
-            raw = keep.tile([P, 2 * H], U8, name="w_raw%d" % j, align_bytes=64)
-            nc.sync.dma_start(raw[:].bitcast(I32), words[0].bitcast(I32))
-            w_raw.append(raw)
-        xw = keep.tile([P, T], U32, name="xw")
-        nc.sync.dma_start(xw[:].bitcast(I32), x_words[0].rearrange("p n t -> p (n t)").bitcast(I32))
-
         xs = keep.tile([P, T], U8, name="xs")
         nc.vector.memset(xs[:].bitcast(I32), 0)
-        ws_raw = [keep.tile([P, H], U8, name="ws_raw%d" % j, tag="late%d" % j, align_bytes=64) for j in range(2)]
-        nc.vector.memset(ws_raw[0][:].bitcast(I32), 0)
-        nc.gpsimd.memset(ws_raw[1][:].bitcast(I32), 0)
+        ident_made = keep.tile([P, P], F32, name="ident_made", tag="xw")
+        make_identity(nc, ident_made[:])
+        ident = keep.tile([P, P], F32, name="ident")
+        nc.vector.tensor_copy(ident[:], ident_made[:])
 
         def load_scale_rows(queue, plane, scales, q):
             queue.dma_start(plane[32 * q : 32 * q + 4, :].bitcast(I32), scales[0, 4 * q : 4 * q + 4, :].bitcast(I32))
 
         for q in range(4):
-            load_scale_rows(nc.scalar, xs, x_scales, q)
+            load_scale_rows(nc.sync, xs, x_scales, q)
+        xw = keep.tile([P, T], U32, name="xw", tag="xw")
+        nc.sync.dma_start(xw[:].bitcast(I32), x_words[0].rearrange("p n t -> p (n t)").bitcast(I32))
+
+        w_raw = []
+        for j, words in enumerate((w1_words, w2_words)):
+            raw = keep.tile([P, 2 * H], U8, name="w_raw%d" % j, align_bytes=64)
+            nc.gpsimd.dma_start(raw[:].bitcast(I32), words[0].bitcast(I32))
+            w_raw.append(raw)
+        ws_raw = [keep.tile([P, H], U8, name="ws_raw%d" % j, tag="late%d" % j, align_bytes=64) for j in range(2)]
+        for j in range(2):
+            nc.gpsimd.memset(ws_raw[j][:].bitcast(I32), 0)
         for q in range(4):
-            load_scale_rows(nc.gpsimd, ws_raw[1], w2_scales, q)
+            load_scale_rows(nc.scalar, ws_raw[1], w2_scales, q)
         for q in range(4):
             load_scale_rows(nc.scalar if q < 3 else nc.gpsimd, ws_raw[0], w1_scales, q)
 
-        ident = keep.tile([P, P], F32, name="ident")
-        make_identity(nc, ident[:])
         two = keep.tile([P, 1], F32, name="two")
         nc.gpsimd.memset(two[:], 2.0)
         tables = []
@@ -89,13 +91,13 @@ def tile_picked_ymuver_rel_p_kernel(
 
         gather_scales(0)
         ws_dealt = [keep.tile([P, SLOTS, P], U8, name="ws_dealt%d" % j, align_bytes=64) for j in range(2)]
-        for j in range(2):
-            nc.vector.tensor_copy(ws_dealt[j][:], ws_raw[j][:].rearrange("p (m t) -> p t m", t=SLOTS))
+        for slots in (slice(0, 1), slice(1, SLOTS)):
+            for j in (1, 0):
+                nc.vector.tensor_copy(ws_dealt[j][:, slots, :], ws_raw[j][:].rearrange("p (m t) -> p t m", t=SLOTS)[:, slots, :])
 
-        q_flat = [keep.tile([P, SLOTS * U + SLOTS], F32, name="q%d" % j, tag="late%d" % j, align_bytes=64) for j in range(2)]
+        q_flat = [keep.tile([P, SLOTS * U + (SLOTS if j == 0 else 0)], F32, name="q%d" % j, tag="late%d" % j, align_bytes=64) for j in range(2)]
         q_t = [flat[:, : SLOTS * U].rearrange("p (t r) -> p t r", t=SLOTS) for flat in q_flat]
         unit_t = q_flat[0][:, SLOTS * U :]
-        neg_unit = q_flat[1][:, SLOTS * U :]
         nc.sync.dma_start(unit_t, unit.rearrange("(p t) o -> p (t o)", t=SLOTS))
         for pair in range(2):
             for j, q_in in enumerate((qa, qb)):
@@ -103,7 +105,6 @@ def tile_picked_ymuver_rel_p_kernel(
                 nc.sync.dma_start(q_t[j][:, rows, :], q_in.rearrange("(p t) r -> p t r", t=SLOTS)[:, rows, :])
         w3w = keep.tile([P, 2 * N], U8, name="w3w", tag="late2", align_bytes=64)
         nc.sync.dma_start(w3w[:].bitcast(I32), w3_words[0].bitcast(I32))
-        nc.vector.tensor_scalar(neg_unit, unit_t, -1.0, None, ALU.mult)
 
         gw = [keep.tile([P, D, P], U32, name="gw%d" % h, align_bytes=64) for h in range(2)]
 
@@ -139,11 +140,16 @@ def tile_picked_ymuver_rel_p_kernel(
                     rhs=gw[h][:, d, :].bitcast(FP8X4), rhs_scale=gs_dealt[h][:, d, :], start=(d == 0), stop=(d == D - 1),
                 )
 
-        def gate(y_bank, yb_bank, last):
-            pool = keep if last else work
-            th = pool.tile([P, D, P], F32, name="th", tag="last_tanh" if last else "th")
+        def gate(y_bank, yb_bank, t, h):
+            if t == SLOTS - 1 and h == 1:
+                th = keep.tile([P, D, P], F32, name="th_last", tag="before_products")
+            else:
+                th = work.tile([P, D, P], F32, name="th")
             nc.scalar.activation(th[:], yb_bank[:], ACT.Tanh)
-            ya2 = work.tile([P, D, P], F32, name="ya2", bufs=3)
+            if t == SLOTS - 1 and h == 1:
+                ya2 = keep.tile([P, D, P], F32, name="ya2_last", tag="before_roots")
+            else:
+                ya2 = work.tile([P, D, P], F32, name="ya2", bufs=3)
             nc.vector.scalar_tensor_tensor(flat(ya2), flat(th), 1.0, flat(y_bank), ALU.add, ALU.mult)
             return ya2
 
@@ -167,7 +173,7 @@ def tile_picked_ymuver_rel_p_kernel(
                         rhs=flat(gw[h]).bitcast(FP8X4), rhs_scale=flat(gs_dealt[h]), start=True, stop=True,
                     )
                 sum_of_products(acc[:, V + h * P : V + (h + 1) * P], 0, h)
-                ya2 = gate(y_bank, yb_bank, False)
+                ya2 = gate(y_bank, yb_bank, 0, h)
                 nc.vector.tensor_tensor(pairs[:, h], ya2[:, 0:2, :], ya2[:, 2:4, :], ALU.add)
             nc.vector.tensor_tensor(
                 tables[0][:, :V].rearrange("p (h v) -> p h v", h=2), pairs[:, :, 0, :], pairs[:, :, 1, :], ALU.add
@@ -186,7 +192,7 @@ def tile_picked_ymuver_rel_p_kernel(
                 else:
                     y_copy = work.tile([P, D, P], F32, name="y_copy")
                     nc.scalar.copy(y_copy[:], y_bank[:])
-                ya2 = gate(y_bank, yb_bank, t == SLOTS - 1 and h == 1)
+                ya2 = gate(y_bank, yb_bank, t, h)
                 if t != 1:
                     sum_turned(y_sum, y_copy)
                 sum_turned(acc[:, h * P : (h + 1) * P], ya2)
@@ -206,26 +212,30 @@ def tile_picked_ymuver_rel_p_kernel(
             mag = work.tile([P, 2, width], F32, name="mag")
             for j in range(2):
                 nc.scalar.activation(mag[:, j, :], g[:, j, :], ACT.Abs)
-            den = keep.tile([P, width], F32, name="den%d_%d" % (t, halves[0]))
-            nc.vector.tensor_tensor(den[:], mag[:, 0, :], mag[:, 1, :], ALU.add)
-            dens[(t, halves[0])] = den
-            prod = work.tile([P, 2, width], F32, name="prod")
-            for j, factor in enumerate((unit_t, neg_unit)):
+            if t == 1:
+                prod = keep.tile([P, 2, width], F32, name="prod_held", tag="before_products")
+            else:
+                prod = work.tile([P, 2, width], F32, name="prod")
+            for j in range(2):
                 nc.vector.scalar_tensor_tensor(
-                    prod[:, j, :], g[:, j, :], factor[:, t : t + 1], q_t[j][:, t, r0 : r0 + width], ALU.mult, ALU.mult
+                    prod[:, j, :], g[:, j, :], unit_t[:, t : t + 1], q_t[j][:, t, r0 : r0 + width], ALU.mult, ALU.mult
                 )
-            nc.vector.tensor_tensor(
+            adder = nc.vector if t == SLOTS - 1 else nc.gpsimd
+            den = keep.tile([P, width], F32, name="den%d_%d" % (t, halves[0]))
+            adder.tensor_tensor(den[:], mag[:, 0, :], mag[:, 1, :], ALU.add)
+            dens[(t, halves[0])] = den
+            adder.tensor_tensor(
                 z[:, halves[0] : halves[-1] + 1, t, :],
                 prod[:, 0, :].rearrange("p (h r) -> p h r", r=HALF),
                 prod[:, 1, :].rearrange("p (h r) -> p h r", r=HALF),
-                ALU.add,
+                ALU.subtract,
             )
 
         def invert(t, halves):
             width = len(halves) * HALF
             first = t == 0
             pool = keep if first else work
-            root = pool.tile([P, width], F32, name="root", tag="last_tanh" if first else "root")
+            root = pool.tile([P, width], F32, name="root", tag="before_roots" if first else "root")
             nc.scalar.activation(root[:], dens[(t, halves[0])][:], ACT.Abs_reciprocal_sqrt, bias=two[:])
             nc.scalar.activation(
                 inv[:, halves[0] : halves[-1] + 1, t, :], root[:].rearrange("p (h r) -> p h r", r=HALF), ACT.Square

@@ -37,37 +37,45 @@ def tile_picked_ymuver_rel_p_kernel(
         doc_t = keep.tile([P, U // 16], U16, name="doc_t")
         alt_t = keep.tile([P, U // 16], U16, name="alt_t")
         nc.sync.dma_start(offs_t[:], offs)
-        nc.sync.dma_start(doc_t[:], doc)
-        nc.sync.dma_start(alt_t[:], alt)
+
+        def load_scale_rows(queue, plane, scales):
+            for q in range(4):
+                queue.dma_start(plane[32 * q : 32 * q + 4, :].bitcast(I32), scales[0, 4 * q : 4 * q + 4, :].bitcast(I32))
 
         xs = keep.tile([P, T], U8, name="xs")
         nc.vector.memset(xs[:].bitcast(I32), 0)
-        ident_made = keep.tile([P, P], F32, name="ident_made", tag="xw")
-        make_identity(nc, ident_made[:])
-        ident = keep.tile([P, P], F32, name="ident")
-        nc.vector.tensor_copy(ident[:], ident_made[:])
-
-        def load_scale_rows(queue, plane, scales, q):
-            queue.dma_start(plane[32 * q : 32 * q + 4, :].bitcast(I32), scales[0, 4 * q : 4 * q + 4, :].bitcast(I32))
-
-        for q in range(4):
-            load_scale_rows(nc.sync, xs, x_scales, q)
-        xw = keep.tile([P, T], U32, name="xw", tag="xw")
-        nc.sync.dma_start(xw[:].bitcast(I32), x_words[0].rearrange("p n t -> p (n t)").bitcast(I32))
-
+        load_scale_rows(nc.sync, xs, x_scales)
         w_raw = []
         for j, words in enumerate((w1_words, w2_words)):
-            raw = keep.tile([P, 2 * H], U8, name="w_raw%d" % j, align_bytes=64)
-            nc.gpsimd.dma_start(raw[:].bitcast(I32), words[0].bitcast(I32))
+            raw = keep.tile([P, 2 * H], U8, name="w_raw%d" % j)
+            nc.sync.dma_start(raw[:].bitcast(I32), words[0].bitcast(I32))
             w_raw.append(raw)
-        ws_raw = [keep.tile([P, H], U8, name="ws_raw%d" % j, tag="late%d" % j, align_bytes=64) for j in range(2)]
-        for j in range(2):
-            nc.gpsimd.memset(ws_raw[j][:].bitcast(I32), 0)
-        for q in range(4):
-            load_scale_rows(nc.scalar, ws_raw[1], w2_scales, q)
-        for q in range(4):
-            load_scale_rows(nc.scalar if q < 3 else nc.gpsimd, ws_raw[0], w1_scales, q)
+        xw = keep.tile([P, T], U32, name="xw")
+        nc.sync.dma_start(xw[:].bitcast(I32), x_words[0].rearrange("p n t -> p (n t)").bitcast(I32))
 
+        ws_raw = [keep.tile([P, H], U8, name="ws_raw%d" % j, tag="ws_raw%d" % j, align_bytes=64) for j in range(2)]
+        for j in (1, 0):
+            nc.gpsimd.memset(ws_raw[j][:].bitcast(I32), 0)
+        load_scale_rows(nc.gpsimd, ws_raw[1], w2_scales)
+        load_scale_rows(nc.sync, ws_raw[0], w1_scales)
+        nc.sync.dma_start(doc_t[:], doc)
+        nc.sync.dma_start(alt_t[:], alt)
+
+        unit_t = keep.tile([P, SLOTS], F32, name="unit_t")
+        nc.sync.dma_start(unit_t[:], unit.rearrange("(p t) o -> p (t o)", t=SLOTS))
+        q_t = [keep.tile([P, SLOTS, U], F32, name="q%d" % j) for j in range(2)]
+        for pair in range(2):
+            for j, q_in in enumerate((qa, qb)):
+                rows = slice(2 * pair, 2 * pair + 2)
+                nc.sync.dma_start(q_t[j][:, rows, :], q_in.rearrange("(p t) r -> p t r", t=SLOTS)[:, rows, :])
+        w3w = keep.tile([P, 2 * N], U8, name="w3w", align_bytes=64)
+        nc.sync.dma_start(w3w[:].bitcast(I32), w3_words[0].bitcast(I32))
+        w3s = keep.tile([P, N], U8, name="w3s", align_bytes=64)
+        nc.gpsimd.memset(w3s[:].bitcast(I32), 0)
+        load_scale_rows(nc.sync, w3s, w3_scales)
+
+        ident = keep.tile([P, P], F32, name="ident")
+        make_identity(nc, ident[:])
         two = keep.tile([P, 1], F32, name="two")
         nc.gpsimd.memset(two[:], 2.0)
         tables = []
@@ -85,28 +93,18 @@ def tile_picked_ymuver_rel_p_kernel(
         gs_dealt = [keep.tile([P, D, P], U8, name="gs_dealt%d" % h, align_bytes=64) for h in range(2)]
 
         def gather_scales(h):
-            gs = keep.tile([P, S // 2], U8, name="gs%d" % h, tag="late%d" % (2 + h), align_bytes=64)
+            gs = keep.tile([P, S // 2], U8, name="gs%d" % h, tag="gs%d" % h, align_bytes=64)
             nc.vector.tensor_copy(gs[:], xs[:].indirect(offs_t[:, 32 * h : 32 * (h + 1)]))
             nc.vector.tensor_copy(gs_dealt[h][:], gs[:].rearrange("p (v d) -> p d v", d=D))
 
         gather_scales(0)
-        ws_dealt = [keep.tile([P, SLOTS, P], U8, name="ws_dealt%d" % j, align_bytes=64) for j in range(2)]
+        gather_scales(1)
+        ws_dealt = [keep.tile([P, SLOTS, P], U8, name="ws_dealt%d" % j, tag="gs%d" % j, align_bytes=64) for j in range(2)]
         for slots in (slice(0, 1), slice(1, SLOTS)):
             for j in (1, 0):
                 nc.vector.tensor_copy(ws_dealt[j][:, slots, :], ws_raw[j][:].rearrange("p (m t) -> p t m", t=SLOTS)[:, slots, :])
 
-        q_flat = [keep.tile([P, SLOTS * U + (SLOTS if j == 0 else 0)], F32, name="q%d" % j, tag="late%d" % j, align_bytes=64) for j in range(2)]
-        q_t = [flat[:, : SLOTS * U].rearrange("p (t r) -> p t r", t=SLOTS) for flat in q_flat]
-        unit_t = q_flat[0][:, SLOTS * U :]
-        nc.sync.dma_start(unit_t, unit.rearrange("(p t) o -> p (t o)", t=SLOTS))
-        for pair in range(2):
-            for j, q_in in enumerate((qa, qb)):
-                rows = slice(2 * pair, 2 * pair + 2)
-                nc.sync.dma_start(q_t[j][:, rows, :], q_in.rearrange("(p t) r -> p t r", t=SLOTS)[:, rows, :])
-        w3w = keep.tile([P, 2 * N], U8, name="w3w", tag="late2", align_bytes=64)
-        nc.sync.dma_start(w3w[:].bitcast(I32), w3_words[0].bitcast(I32))
-
-        gw = [keep.tile([P, D, P], U32, name="gw%d" % h, align_bytes=64) for h in range(2)]
+        gw = [keep.tile([P, D, P], U32, name="gw%d" % h, tag="ws_raw%d" % (1 - h), align_bytes=64) for h in range(2)]
 
         def gather_words(h):
             nc.vector.tensor_copy(gw[h][:].rearrange("p d v -> p v d"), xw[:].indirect(offs_t[:, 32 * h : 32 * (h + 1)]))
@@ -154,7 +152,7 @@ def tile_picked_ymuver_rel_p_kernel(
             return ya2
 
         def banks():
-            return psum.tile([P, D, P], F32, name="y_bank", bufs=3), psum.tile([P, D, P], F32, name="yb_bank", bufs=2)
+            return psum.tile([P, D, P], F32, name="y_bank", bufs=3), psum.tile([P, D, P], F32, name="yb_bank", tag="yb_bank", bufs=3)
 
         def other_side(t, acc):
             nc.vector.scalar_tensor_tensor(tables[t][:, V : 2 * V], acc[:, V:], -2.0, tables[t][:, :V], ALU.mult, ALU.add)
@@ -163,8 +161,6 @@ def tile_picked_ymuver_rel_p_kernel(
             acc = psum.tile([P, 2 * V], F32, name="acc", bufs=2)
             pairs = keep.tile([P, 2, 2, P], F32, name="pairs")
             for h in range(2):
-                if h == 1:
-                    gather_scales(h)
                 gather_words(h)
                 y_bank, yb_bank = banks()
                 for j, bank in ((1, yb_bank), (0, y_bank)):
@@ -220,7 +216,7 @@ def tile_picked_ymuver_rel_p_kernel(
                 nc.vector.scalar_tensor_tensor(
                     prod[:, j, :], g[:, j, :], unit_t[:, t : t + 1], q_t[j][:, t, r0 : r0 + width], ALU.mult, ALU.mult
                 )
-            adder = nc.vector if t == SLOTS - 1 else nc.gpsimd
+            adder = nc.vector
             den = keep.tile([P, width], F32, name="den%d_%d" % (t, halves[0]))
             adder.tensor_tensor(den[:], mag[:, 0, :], mag[:, 1, :], ALU.add)
             dens[(t, halves[0])] = den
@@ -241,8 +237,6 @@ def tile_picked_ymuver_rel_p_kernel(
                 inv[:, halves[0] : halves[-1] + 1, t, :], root[:].rearrange("p (h r) -> p h r", r=HALF), ACT.Square
             )
 
-        out_bank = psum.tile([P, U], F32, name="out_bank")
-
         def project(h):
             hid = work.tile([P, HALF, SLOTS], BF16, name="hid", align_bytes=64)
             nc.vector.tensor_tensor(
@@ -255,20 +249,17 @@ def tile_picked_ymuver_rel_p_kernel(
             scales = work.tile([P, HALF], U8, name="scales", align_bytes=64)
             nc.vector.quantize_mx(out=codes[:].bitcast(FP8X4), scales=scales[:], in_=hid[:].rearrange("p r t -> p (r t)"))
             cols = slice(h * HALF, (h + 1) * HALF)
+            out_bank = psum.tile([P, HALF], F32, name="out_bank", tag="yb_bank", bufs=3)
             nc.tensor.matmul_mx(
-                out=out_bank[:, cols], lhsT=w3w[:].bitcast(FP4X4), lhsT_scale=w3s[:],
+                out=out_bank[:], lhsT=w3w[:].bitcast(FP4X4), lhsT_scale=w3s[:],
                 rhs=codes[:].bitcast(FP8X4), rhs_scale=scales[:], start=True, stop=True,
             )
             result = work.tile([P, HALF], F32, name="result")
-            nc.scalar.copy(result[:], out_bank[:, cols])
+            nc.scalar.copy(result[:], out_bank[:])
             nc.sync.dma_start(out[:, cols], result[:])
 
         both = (0, 1)
         encode_first()
-        w3s = keep.tile([P, N], U8, name="w3s", tag="late3", align_bytes=64)
-        nc.gpsimd.memset(w3s[:].bitcast(I32), 0)
-        for q in range(4):
-            load_scale_rows(nc.sync, w3s, w3_scales, q)
         for t in range(1, SLOTS):
             encode(t)
         look_up(0, both)

@@ -19,8 +19,13 @@ ALU = mybir.AluOpType
 
 P = 128
 SLOTS = 4
+LAST = SLOTS - 1
+PER_COLUMN = 16
+GROUPS = V // P
 HALF = U // 2
-WINDOW = 768
+WINDOW = 3 * V
+LINE = 4
+W1, W2 = 0, 1
 
 
 def tile_picked_ymuver_rel_p_kernel(
@@ -33,14 +38,14 @@ def tile_picked_ymuver_rel_p_kernel(
         work = ctx.enter_context(tc.tile_pool(name="work", bufs=2))
         psum = ctx.enter_context(tc.psum_pool(name="psum", bufs=1))
 
-        offs_t = keep.tile([P, S // 16], U16, name="offs_t")
-        doc_t = keep.tile([P, U // 16], U16, name="doc_t")
-        alt_t = keep.tile([P, U // 16], U16, name="alt_t")
+        offs_t = keep.tile([P, S // PER_COLUMN], U16, name="offs_t")
+        doc_t = keep.tile([P, U // PER_COLUMN], U16, name="doc_t")
+        alt_t = keep.tile([P, U // PER_COLUMN], U16, name="alt_t")
         nc.sync.dma_start(offs_t[:], offs)
 
-        def load_scale_rows(queue, plane, scales):
+        def load_scale_rows(queue, rows, scales):
             for q in range(4):
-                queue.dma_start(plane[32 * q : 32 * q + 4, :].bitcast(I32), scales[0, 4 * q : 4 * q + 4, :].bitcast(I32))
+                queue.dma_start(rows[32 * q : 32 * q + 4, :].bitcast(I32), scales[0, 4 * q : 4 * q + 4, :].bitcast(I32))
 
         xs = keep.tile([P, T], U8, name="xs")
         nc.vector.memset(xs[:].bitcast(I32), 0)
@@ -53,21 +58,21 @@ def tile_picked_ymuver_rel_p_kernel(
         xw = keep.tile([P, T], U32, name="xw")
         nc.sync.dma_start(xw[:].bitcast(I32), x_words[0].rearrange("p n t -> p (n t)").bitcast(I32))
 
-        ws_raw = [keep.tile([P, H], U8, name="ws_raw%d" % j, tag="ws_raw%d" % j, align_bytes=64) for j in range(2)]
-        for j in (1, 0):
+        ws_raw = [keep.tile([P, H], U8, name="ws_raw%d" % j, tag="ws_raw%d" % j, align_bytes=64) for j in (W1, W2)]
+        for j in (W2, W1):
             nc.gpsimd.memset(ws_raw[j][:].bitcast(I32), 0)
-        load_scale_rows(nc.gpsimd, ws_raw[1], w2_scales)
-        load_scale_rows(nc.sync, ws_raw[0], w1_scales)
+        load_scale_rows(nc.gpsimd, ws_raw[W2], w2_scales)
+        load_scale_rows(nc.sync, ws_raw[W1], w1_scales)
         nc.sync.dma_start(doc_t[:], doc)
         nc.sync.dma_start(alt_t[:], alt)
 
         unit_t = keep.tile([P, SLOTS], F32, name="unit_t")
         nc.sync.dma_start(unit_t[:], unit.rearrange("(p t) o -> p (t o)", t=SLOTS))
-        q_t = [keep.tile([P, SLOTS, U], F32, name="q%d" % j) for j in range(2)]
-        for pair in range(2):
-            for j, q_in in enumerate((qa, qb)):
-                rows = slice(2 * pair, 2 * pair + 2)
-                nc.sync.dma_start(q_t[j][:, rows, :], q_in.rearrange("(p t) r -> p t r", t=SLOTS)[:, rows, :])
+        q_t = [keep.tile([P, SLOTS, U], F32, name="q%d" % side) for side in range(2)]
+        for first in range(0, SLOTS, 2):
+            for side, q_in in enumerate((qa, qb)):
+                slots = slice(first, first + 2)
+                nc.sync.dma_start(q_t[side][:, slots, :], q_in.rearrange("(p t) r -> p t r", t=SLOTS)[:, slots, :])
         w3w = keep.tile([P, 2 * N], U8, name="w3w", align_bytes=64)
         nc.sync.dma_start(w3w[:].bitcast(I32), w3_words[0].bitcast(I32))
         w3s = keep.tile([P, N], U8, name="w3s", align_bytes=64)
@@ -80,46 +85,37 @@ def tile_picked_ymuver_rel_p_kernel(
         nc.gpsimd.memset(two[:], 2.0)
         tables = []
         for t in range(SLOTS):
-            table = keep.tile([P, 4 * V], F32, name="table%d" % t)
+            table = keep.tile([P, V + WINDOW], F32, name="table%d" % t)
             nc.gpsimd.memset(table[:, 2 * V :], 0.0)
             tables.append(table)
 
         w_dealt = []
-        for j in range(2):
+        for j in (W1, W2):
             dealt = keep.tile([P, SLOTS, P, 2], U8, name="w_dealt%d" % j, align_bytes=64)
             nc.vector.tensor_copy(dealt[:], w_raw[j][:].rearrange("p (m t b) -> p t m b", t=SLOTS, b=2))
             w_dealt.append(dealt)
 
-        gs_dealt = [keep.tile([P, D, P], U8, name="gs_dealt%d" % h, align_bytes=64) for h in range(2)]
+        def group_offsets(g):
+            columns = P * D // PER_COLUMN
+            return offs_t[:, g * columns : (g + 1) * columns]
 
-        def gather_scales(h):
-            gs = keep.tile([P, S // 2], U8, name="gs%d" % h, tag="gs%d" % h, align_bytes=64)
-            nc.vector.tensor_copy(gs[:], xs[:].indirect(offs_t[:, 32 * h : 32 * (h + 1)]))
-            nc.vector.tensor_copy(gs_dealt[h][:], gs[:].rearrange("p (v d) -> p d v", d=D))
+        gs_dealt = [keep.tile([P, D, P], U8, name="gs_dealt%d" % g, align_bytes=64) for g in range(GROUPS)]
+        for g in range(GROUPS):
+            gs = keep.tile([P, P * D], U8, name="gs%d" % g, tag="gs%d" % g, align_bytes=64)
+            nc.vector.tensor_copy(gs[:], xs[:].indirect(group_offsets(g)))
+            nc.vector.tensor_copy(gs_dealt[g][:], gs[:].rearrange("p (v d) -> p d v", d=D))
 
-        gather_scales(0)
-        gather_scales(1)
-        ws_dealt = [keep.tile([P, SLOTS, P], U8, name="ws_dealt%d" % j, tag="gs%d" % j, align_bytes=64) for j in range(2)]
+        ws_dealt = [keep.tile([P, SLOTS, P], U8, name="ws_dealt%d" % j, tag="gs%d" % j, align_bytes=64) for j in (W1, W2)]
         for slots in (slice(0, 1), slice(1, SLOTS)):
-            for j in (1, 0):
+            for j in (W2, W1):
                 nc.vector.tensor_copy(ws_dealt[j][:, slots, :], ws_raw[j][:].rearrange("p (m t) -> p t m", t=SLOTS)[:, slots, :])
 
-        gw = [keep.tile([P, D, P], U32, name="gw%d" % h, tag="ws_raw%d" % (1 - h), align_bytes=64) for h in range(2)]
+        gw = [
+            keep.tile([P, D, P], U32, name="gw%d" % g, tag="ws_raw%d" % j, align_bytes=64) for g, j in enumerate((W2, W1))
+        ]
 
-        def gather_words(h):
-            nc.vector.tensor_copy(gw[h][:].rearrange("p d v -> p v d"), xw[:].indirect(offs_t[:, 32 * h : 32 * (h + 1)]))
-
-        def products(bank, j, t, h):
-            for d in range(D):
-                nc.tensor.matmul_mx(
-                    out=bank[:, d, :],
-                    lhsT=gw[h][:, d, :].bitcast(FP8X4),
-                    lhsT_scale=gs_dealt[h][:, d, :],
-                    rhs=weights(j, t),
-                    rhs_scale=ws_dealt[j][:, t, :],
-                    start=True,
-                    stop=True,
-                )
+        def gather_words(g):
+            nc.vector.tensor_copy(gw[g][:].rearrange("p d v -> p v d"), xw[:].indirect(group_offsets(g)))
 
         def flat(tile):
             return tile[:].rearrange("p a b -> p (a b)")
@@ -127,128 +123,142 @@ def tile_picked_ymuver_rel_p_kernel(
         def weights(j, t):
             return w_dealt[j][:, t].rearrange("p m b -> p (m b)").bitcast(FP4X4)
 
-        def sum_turned(target, part):
-            for d in range(D):
-                nc.tensor.matmul(target, lhsT=part[:, d, :], rhs=ident[:], is_transpose=True, start=(d == 0), stop=(d == D - 1))
+        def product_by_feature(bank, j, g):
+            nc.tensor.matmul_mx(
+                out=flat(bank), lhsT=weights(j, 0), lhsT_scale=ws_dealt[j][:, 0, :],
+                rhs=flat(gw[g]).bitcast(FP8X4), rhs_scale=flat(gs_dealt[g]), start=True, stop=True,
+            )
 
-        def sum_of_products(target, t, h):
+        def product_by_document(bank, j, t, g):
             for d in range(D):
                 nc.tensor.matmul_mx(
-                    out=target, lhsT=weights(0, t), lhsT_scale=ws_dealt[0][:, t, :],
-                    rhs=gw[h][:, d, :].bitcast(FP8X4), rhs_scale=gs_dealt[h][:, d, :], start=(d == 0), stop=(d == D - 1),
+                    out=bank[:, d, :], lhsT=gw[g][:, d, :].bitcast(FP8X4), lhsT_scale=gs_dealt[g][:, d, :],
+                    rhs=weights(j, t), rhs_scale=ws_dealt[j][:, t, :], start=True, stop=True,
                 )
 
-        def gate(y_bank, yb_bank, t, h):
-            if t == SLOTS - 1 and h == 1:
-                th = keep.tile([P, D, P], F32, name="th_last", tag="before_products")
+        def sum_y_by_passes(target, t, g):
+            for d in range(D):
+                nc.tensor.matmul_mx(
+                    out=target, lhsT=weights(W1, t), lhsT_scale=ws_dealt[W1][:, t, :],
+                    rhs=gw[g][:, d, :].bitcast(FP8X4), rhs_scale=gs_dealt[g][:, d, :], start=(d == 0), stop=(d == D - 1),
+                )
+
+        def sum_by_transposes(target, values):
+            for d in range(D):
+                nc.tensor.matmul(target, lhsT=values[:, d, :], rhs=ident[:], is_transpose=True, start=(d == 0), stop=(d == D - 1))
+
+        tanhs = {}
+
+        def tanh_tag(t, g):
+            return "tanh%d_%d" % (t, g)
+
+        def squash(t, g):
+            yb_bank = psum.tile([P, D, P], F32, name="yb_bank", tag="yb_bank", bufs=3)
+            if t == 0:
+                product_by_feature(yb_bank, W2, g)
             else:
-                th = work.tile([P, D, P], F32, name="th")
-            nc.scalar.activation(th[:], yb_bank[:], ACT.Tanh)
-            if t == SLOTS - 1 and h == 1:
-                ya2 = keep.tile([P, D, P], F32, name="ya2_last", tag="before_roots")
-            else:
-                ya2 = work.tile([P, D, P], F32, name="ya2", bufs=3)
-            nc.vector.scalar_tensor_tensor(flat(ya2), flat(th), 1.0, flat(y_bank), ALU.add, ALU.mult)
+                product_by_document(yb_bank, W2, t, g)
+            tanhs[(t, g)] = keep.tile([P, D, P], F32, name="tanh_yb", tag=tanh_tag(t, g))
+            nc.scalar.activation(tanhs[(t, g)][:], yb_bank[:], ACT.Tanh)
+
+        def gate(y_bank, t, g):
+            ya2 = work.tile([P, D, P], F32, name="ya2", bufs=3)
+            nc.vector.scalar_tensor_tensor(flat(ya2), flat(tanhs[(t, g)]), 1.0, flat(y_bank), ALU.add, ALU.mult)
             return ya2
 
-        def banks():
-            return psum.tile([P, D, P], F32, name="y_bank", bufs=3), psum.tile([P, D, P], F32, name="yb_bank", tag="yb_bank", bufs=3)
-
-        def other_side(t, acc):
-            nc.vector.scalar_tensor_tensor(tables[t][:, V : 2 * V], acc[:, V:], -2.0, tables[t][:, :V], ALU.mult, ALU.add)
+        def other_side(t, sums):
+            nc.vector.scalar_tensor_tensor(tables[t][:, V : 2 * V], sums[:, V:], -2.0, tables[t][:, :V], ALU.mult, ALU.add)
 
         def encode_first():
-            acc = psum.tile([P, 2 * V], F32, name="acc", bufs=2)
-            pairs = keep.tile([P, 2, 2, P], F32, name="pairs")
-            for h in range(2):
-                gather_words(h)
-                y_bank, yb_bank = banks()
-                for j, bank in ((1, yb_bank), (0, y_bank)):
-                    nc.tensor.matmul_mx(
-                        out=flat(bank), lhsT=weights(j, 0), lhsT_scale=ws_dealt[j][:, 0, :],
-                        rhs=flat(gw[h]).bitcast(FP8X4), rhs_scale=flat(gs_dealt[h]), start=True, stop=True,
-                    )
-                sum_of_products(acc[:, V + h * P : V + (h + 1) * P], 0, h)
-                ya2 = gate(y_bank, yb_bank, 0, h)
-                nc.vector.tensor_tensor(pairs[:, h], ya2[:, 0:2, :], ya2[:, 2:4, :], ALU.add)
+            sums = psum.tile([P, 2 * V], F32, name="sums", bufs=2)
+            pairs = keep.tile([P, GROUPS, 2, P], F32, name="pairs")
+            for g in range(GROUPS):
+                gather_words(g)
+                squash(0, g)
+                y_bank = psum.tile([P, D, P], F32, name="y_bank", bufs=3)
+                product_by_feature(y_bank, W1, g)
+                sum_y_by_passes(sums[:, V + g * P : V + (g + 1) * P], 0, g)
+                ya2 = gate(y_bank, 0, g)
+                nc.vector.tensor_tensor(pairs[:, g], ya2[:, 0:2, :], ya2[:, 2:4, :], ALU.add)
             nc.vector.tensor_tensor(
-                tables[0][:, :V].rearrange("p (h v) -> p h v", h=2), pairs[:, :, 0, :], pairs[:, :, 1, :], ALU.add
+                tables[0][:, :V].rearrange("p (g v) -> p g v", g=GROUPS), pairs[:, :, 0, :], pairs[:, :, 1, :], ALU.add
             )
-            other_side(0, acc)
+            other_side(0, sums)
 
         def encode(t):
-            acc = psum.tile([P, 2 * V], F32, name="acc", bufs=2)
-            for h in range(2):
-                y_bank, yb_bank = banks()
-                products(y_bank, 0, t, h)
-                products(yb_bank, 1, t, h)
-                y_sum = acc[:, V + h * P : V + (h + 1) * P]
-                if t == 1:
-                    sum_of_products(y_sum, t, h)
+            sums = psum.tile([P, 2 * V], F32, name="sums", bufs=2)
+            by_passes = t == 1
+            for g in range(GROUPS):
+                y_bank = psum.tile([P, D, P], F32, name="y_bank", bufs=3)
+                product_by_document(y_bank, W1, t, g)
+                y_sum = sums[:, V + g * P : V + (g + 1) * P]
+                if by_passes:
+                    sum_y_by_passes(y_sum, t, g)
                 else:
                     y_copy = work.tile([P, D, P], F32, name="y_copy")
                     nc.scalar.copy(y_copy[:], y_bank[:])
-                ya2 = gate(y_bank, yb_bank, t, h)
-                if t != 1:
-                    sum_turned(y_sum, y_copy)
-                sum_turned(acc[:, h * P : (h + 1) * P], ya2)
-            nc.scalar.copy(tables[t][:, :V], acc[:, :V])
-            other_side(t, acc)
+                ya2 = gate(y_bank, t, g)
+                if not by_passes:
+                    sum_by_transposes(y_sum, y_copy)
+                sum_by_transposes(sums[:, g * P : (g + 1) * P], ya2)
+            nc.scalar.copy(tables[t][:, :V], sums[:, :V])
+            other_side(t, sums)
 
-        z = keep.tile([P, 2, SLOTS, HALF], F32, name="z")
+        numer = keep.tile([P, 2, SLOTS, HALF], F32, name="numer")
         inv = keep.tile([P, 2, SLOTS, HALF], F32, name="inv")
-        dens = {}
 
-        def look_up(t, halves):
-            r0, width = halves[0] * HALF, len(halves) * HALF
-            cols = slice(r0 // 16, (r0 + width) // 16)
-            g = work.tile([P, 2, width], F32, name="g")
-            nc.vector.tensor_copy(g[:, 0, :], tables[t][:, 0:WINDOW].indirect(doc_t[:, cols]))
-            nc.vector.tensor_copy(g[:, 1, :], tables[t][:, V : V + WINDOW].indirect(alt_t[:, cols]))
+        def by_half(values):
+            return values.rearrange("p (h r) -> p h r", r=HALF)
+
+        def look_up(t):
+            found = work.tile([P, 2, U], F32, name="found")
+            nc.vector.tensor_copy(found[:, 0, :], tables[t][:, 0:WINDOW].indirect(doc_t[:]))
+            nc.vector.tensor_copy(found[:, 1, :], tables[t][:, V : V + WINDOW].indirect(alt_t[:]))
+            return found
+
+        def terms(t, found, cols, tag):
+            width = cols.stop - cols.start
             mag = work.tile([P, 2, width], F32, name="mag")
-            for j in range(2):
-                nc.scalar.activation(mag[:, j, :], g[:, j, :], ACT.Abs)
-            if t == 1:
-                prod = keep.tile([P, 2, width], F32, name="prod_held", tag="before_products")
-            else:
-                prod = work.tile([P, 2, width], F32, name="prod")
-            for j in range(2):
+            for side in range(2):
+                nc.scalar.activation(mag[:, side, :], found[:, side, cols], ACT.Abs)
+            prod = keep.tile([P, 2, width], F32, name="prod", tag=tag)
+            for side in range(2):
                 nc.vector.scalar_tensor_tensor(
-                    prod[:, j, :], g[:, j, :], unit_t[:, t : t + 1], q_t[j][:, t, r0 : r0 + width], ALU.mult, ALU.mult
+                    prod[:, side, :], found[:, side, cols], unit_t[:, t : t + 1], q_t[side][:, t, cols], ALU.mult, ALU.mult
                 )
-            adder = nc.vector
-            den = keep.tile([P, width], F32, name="den%d_%d" % (t, halves[0]))
-            adder.tensor_tensor(den[:], mag[:, 0, :], mag[:, 1, :], ALU.add)
-            dens[(t, halves[0])] = den
-            adder.tensor_tensor(
-                z[:, halves[0] : halves[-1] + 1, t, :],
-                prod[:, 0, :].rearrange("p (h r) -> p h r", r=HALF),
-                prod[:, 1, :].rearrange("p (h r) -> p h r", r=HALF),
-                ALU.subtract,
-            )
+            return mag, prod
 
-        def invert(t, halves):
-            width = len(halves) * HALF
-            first = t == 0
-            pool = keep if first else work
-            root = pool.tile([P, width], F32, name="root", tag="before_roots" if first else "root")
-            nc.scalar.activation(root[:], dens[(t, halves[0])][:], ACT.Abs_reciprocal_sqrt, bias=two[:])
-            nc.scalar.activation(
-                inv[:, halves[0] : halves[-1] + 1, t, :], root[:].rearrange("p (h r) -> p h r", r=HALF), ACT.Square
-            )
+        def invert(target, den, width):
+            root = work.tile([P, width], F32, name="root")
+            nc.scalar.activation(root[:], den, ACT.Abs_reciprocal_sqrt, bias=two[:])
+            nc.scalar.activation(target, by_half(root[:]), ACT.Square)
+
+        def combine(t):
+            tag = tanh_tag(LAST, GROUPS - 1) if t == LAST - 1 else "prod%d" % t
+            mag, prod = terms(t, look_up(t), slice(0, U), tag)
+            nc.gpsimd.tensor_tensor(numer[:, :, t, :], by_half(prod[:, 0, :]), by_half(prod[:, 1, :]), ALU.subtract)
+            den = prod[:, 0, :]
+            nc.gpsimd.tensor_tensor(den, mag[:, 0, :], mag[:, 1, :], ALU.add)
+            invert(inv[:, :, t, :], den, U)
+
+        def combine_last(found, h):
+            mag, prod = terms(LAST, found, slice(h * HALF, (h + 1) * HALF), "prod_last%d" % h)
+            den = keep.tile([P, HALF], F32, name="den%d" % h)
+            nc.vector.tensor_tensor(den[:], mag[:, 0, :], mag[:, 1, :], ALU.add)
+            nc.vector.tensor_tensor(numer[:, h : h + 1, LAST, :], by_half(prod[:, 0, :]), by_half(prod[:, 1, :]), ALU.subtract)
+            invert(inv[:, h : h + 1, LAST, :], den[:], HALF)
 
         def project(h):
             hid = work.tile([P, HALF, SLOTS], BF16, name="hid", align_bytes=64)
             nc.vector.tensor_tensor(
-                hid[:].rearrange("p (c i) t -> p c t i", i=4),
-                z[:, h].rearrange("p t (c i) -> p c t i", i=4),
-                inv[:, h].rearrange("p t (c i) -> p c t i", i=4),
+                hid[:].rearrange("p (c i) t -> p c t i", i=LINE),
+                numer[:, h].rearrange("p t (c i) -> p c t i", i=LINE),
+                inv[:, h].rearrange("p t (c i) -> p c t i", i=LINE),
                 ALU.mult,
             )
             codes = work.tile([P, HALF], U32, name="codes", align_bytes=64)
             scales = work.tile([P, HALF], U8, name="scales", align_bytes=64)
-            nc.vector.quantize_mx(out=codes[:].bitcast(FP8X4), scales=scales[:], in_=hid[:].rearrange("p r t -> p (r t)"))
-            cols = slice(h * HALF, (h + 1) * HALF)
+            nc.vector.quantize_mx(out=codes[:].bitcast(FP8X4), scales=scales[:], in_=flat(hid))
             out_bank = psum.tile([P, HALF], F32, name="out_bank", tag="yb_bank", bufs=3)
             nc.tensor.matmul_mx(
                 out=out_bank[:], lhsT=w3w[:].bitcast(FP4X4), lhsT_scale=w3s[:],
@@ -256,21 +266,18 @@ def tile_picked_ymuver_rel_p_kernel(
             )
             result = work.tile([P, HALF], F32, name="result")
             nc.scalar.copy(result[:], out_bank[:])
-            nc.sync.dma_start(out[:, cols], result[:])
+            nc.sync.dma_start(out[:, h * HALF : (h + 1) * HALF], result[:])
 
-        both = (0, 1)
         encode_first()
         for t in range(1, SLOTS):
+            for g in range(GROUPS):
+                squash(t, g)
+        for t in range(1, SLOTS):
             encode(t)
-        look_up(0, both)
-        look_up(1, both)
-        invert(0, both)
-        look_up(2, both)
-        invert(1, both)
-        look_up(3, (0,))
-        invert(2, both)
-        invert(3, (0,))
-        look_up(3, (1,))
-        invert(3, (1,))
-        project(0)
-        project(1)
+        for t in range(LAST):
+            combine(t)
+        found_last = look_up(LAST)
+        for h in range(2):
+            combine_last(found_last, h)
+        for h in range(2):
+            project(h)

from contextlib import ExitStack

import concourse.mybir as mybir
from concourse.masks import make_identity

K, T, S, D, N, H, V, U = 512, 4096, 1024, 4, 128, 512, 256, 512
FLOPS = 2 * K * H * S * 2 + 2 * H * N * U

F32 = mybir.dt.float32
BF16 = mybir.dt.bfloat16
I32 = mybir.dt.int32
U32 = mybir.dt.uint32
U16 = mybir.dt.uint16
U8 = mybir.dt.uint8
FP8X4 = mybir.dt.float8_e4m3fn_x4
FP4X4 = mybir.dt.float4_e2m1fn_x4
ACT = mybir.ActivationFunctionType
ALU = mybir.AluOpType

P = 128
SLOTS = 4
LAST = SLOTS - 1
PER_COLUMN = 16
GROUPS = V // P
HALF = U // 2
WINDOW = 3 * V
LINE = 4
W1, W2 = 0, 1


def tile_picked_ymuver_rel_p_kernel(
    tc, x_words, x_scales, w1_words, w1_scales, w2_words, w2_scales, qa, qb, unit, w3_words, w3_scales,
    offs, doc, alt, out,
):
    nc = tc.nc
    with ExitStack() as ctx:
        keep = ctx.enter_context(tc.tile_pool(name="keep", bufs=1))
        work = ctx.enter_context(tc.tile_pool(name="work", bufs=2))
        psum = ctx.enter_context(tc.psum_pool(name="psum", bufs=1))

        offs_t = keep.tile([P, S // PER_COLUMN], U16, name="offs_t")
        doc_t = keep.tile([P, U // PER_COLUMN], U16, name="doc_t")
        alt_t = keep.tile([P, U // PER_COLUMN], U16, name="alt_t")
        nc.sync.dma_start(offs_t[:], offs)

        def load_scale_rows(queue, rows, scales):
            for q in range(4):
                queue.dma_start(rows[32 * q : 32 * q + 4, :].bitcast(I32), scales[0, 4 * q : 4 * q + 4, :].bitcast(I32))

        xs = keep.tile([P, T], U8, name="xs")
        nc.vector.memset(xs[:].bitcast(I32), 0)
        load_scale_rows(nc.sync, xs, x_scales)
        w_raw = []
        for j, words in enumerate((w1_words, w2_words)):
            raw = keep.tile([P, 2 * H], U8, name="w_raw%d" % j)
            nc.sync.dma_start(raw[:].bitcast(I32), words[0].bitcast(I32))
            w_raw.append(raw)
        xw = keep.tile([P, T], U32, name="xw")
        nc.sync.dma_start(xw[:].bitcast(I32), x_words[0].rearrange("p n t -> p (n t)").bitcast(I32))

        ws_raw = [keep.tile([P, H], U8, name="ws_raw%d" % j, tag="ws_raw%d" % j, align_bytes=64) for j in (W1, W2)]
        for j in (W2, W1):
            nc.gpsimd.memset(ws_raw[j][:].bitcast(I32), 0)
        load_scale_rows(nc.gpsimd, ws_raw[W2], w2_scales)
        load_scale_rows(nc.sync, ws_raw[W1], w1_scales)
        nc.sync.dma_start(doc_t[:], doc)
        nc.sync.dma_start(alt_t[:], alt)

        unit_t = keep.tile([P, SLOTS], F32, name="unit_t")
        nc.sync.dma_start(unit_t[:], unit.rearrange("(p t) o -> p (t o)", t=SLOTS))
        q_t = [keep.tile([P, SLOTS, U], F32, name="q%d" % side) for side in range(2)]
        for first in range(0, SLOTS, 2):
            for side, q_in in enumerate((qa, qb)):
                slots = slice(first, first + 2)
                nc.sync.dma_start(q_t[side][:, slots, :], q_in.rearrange("(p t) r -> p t r", t=SLOTS)[:, slots, :])
        w3w = keep.tile([P, 2 * N], U8, name="w3w", align_bytes=64)
        nc.sync.dma_start(w3w[:].bitcast(I32), w3_words[0].bitcast(I32))
        w3s = keep.tile([P, N], U8, name="w3s", align_bytes=64)
        nc.gpsimd.memset(w3s[:].bitcast(I32), 0)
        load_scale_rows(nc.sync, w3s, w3_scales)

        ident = keep.tile([P, P], F32, name="ident")
        make_identity(nc, ident[:])
        two = keep.tile([P, 1], F32, name="two")
        nc.gpsimd.memset(two[:], 2.0)
        tables = []
        for t in range(SLOTS):
            table = keep.tile([P, V + WINDOW], F32, name="table%d" % t)
            nc.gpsimd.memset(table[:, 2 * V :], 0.0)
            tables.append(table)

        w_dealt = []
        for j in (W1, W2):
            dealt = keep.tile([P, SLOTS, P, 2], U8, name="w_dealt%d" % j, align_bytes=64)
            nc.vector.tensor_copy(dealt[:], w_raw[j][:].rearrange("p (m t b) -> p t m b", t=SLOTS, b=2))
            w_dealt.append(dealt)

        def group_offsets(g):
            columns = P * D // PER_COLUMN
            return offs_t[:, g * columns : (g + 1) * columns]

        gs_dealt = [keep.tile([P, D, P], U8, name="gs_dealt%d" % g, align_bytes=64) for g in range(GROUPS)]
        for g in range(GROUPS):
            gs = keep.tile([P, P * D], U8, name="gs%d" % g, tag="gs%d" % g, align_bytes=64)
            nc.vector.tensor_copy(gs[:], xs[:].indirect(group_offsets(g)))
            nc.vector.tensor_copy(gs_dealt[g][:], gs[:].rearrange("p (v d) -> p d v", d=D))

        ws_dealt = [keep.tile([P, SLOTS, P], U8, name="ws_dealt%d" % j, tag="gs%d" % j, align_bytes=64) for j in (W1, W2)]
        for slots in (slice(0, 1), slice(1, SLOTS)):
            for j in (W2, W1):
                nc.vector.tensor_copy(ws_dealt[j][:, slots, :], ws_raw[j][:].rearrange("p (m t) -> p t m", t=SLOTS)[:, slots, :])

        gw = [
            keep.tile([P, D, P], U32, name="gw%d" % g, tag="ws_raw%d" % j, align_bytes=64) for g, j in enumerate((W2, W1))
        ]

        def gather_words(g):
            nc.vector.tensor_copy(gw[g][:].rearrange("p d v -> p v d"), xw[:].indirect(group_offsets(g)))

        def flat(tile):
            return tile[:].rearrange("p a b -> p (a b)")

        def weights(j, t):
            return w_dealt[j][:, t].rearrange("p m b -> p (m b)").bitcast(FP4X4)

        def product_by_feature(bank, j, g):
            nc.tensor.matmul_mx(
                out=flat(bank), lhsT=weights(j, 0), lhsT_scale=ws_dealt[j][:, 0, :],
                rhs=flat(gw[g]).bitcast(FP8X4), rhs_scale=flat(gs_dealt[g]), start=True, stop=True,
            )

        def product_by_document(bank, j, t, g):
            for d in range(D):
                nc.tensor.matmul_mx(
                    out=bank[:, d, :], lhsT=gw[g][:, d, :].bitcast(FP8X4), lhsT_scale=gs_dealt[g][:, d, :],
                    rhs=weights(j, t), rhs_scale=ws_dealt[j][:, t, :], start=True, stop=True,
                )

        def sum_y_by_passes(target, t, g):
            for d in range(D):
                nc.tensor.matmul_mx(
                    out=target, lhsT=weights(W1, t), lhsT_scale=ws_dealt[W1][:, t, :],
                    rhs=gw[g][:, d, :].bitcast(FP8X4), rhs_scale=gs_dealt[g][:, d, :], start=(d == 0), stop=(d == D - 1),
                )

        def sum_by_transposes(target, values):
            for d in range(D):
                nc.tensor.matmul(target, lhsT=values[:, d, :], rhs=ident[:], is_transpose=True, start=(d == 0), stop=(d == D - 1))

        tanhs = {}

        def tanh_tag(t, g):
            return "tanh%d_%d" % (t, g)

        def squash(t, g):
            yb_bank = psum.tile([P, D, P], F32, name="yb_bank", tag="yb_bank", bufs=3)
            if t == 0:
                product_by_feature(yb_bank, W2, g)
            else:
                product_by_document(yb_bank, W2, t, g)
            tanhs[(t, g)] = keep.tile([P, D, P], F32, name="tanh_yb", tag=tanh_tag(t, g))
            nc.scalar.activation(tanhs[(t, g)][:], yb_bank[:], ACT.Tanh)

        def gate(y_bank, t, g):
            ya2 = work.tile([P, D, P], F32, name="ya2", bufs=3)
            nc.vector.scalar_tensor_tensor(flat(ya2), flat(tanhs[(t, g)]), 1.0, flat(y_bank), ALU.add, ALU.mult)
            return ya2

        def other_side(t, sums):
            nc.vector.scalar_tensor_tensor(tables[t][:, V : 2 * V], sums[:, V:], -2.0, tables[t][:, :V], ALU.mult, ALU.add)

        def encode_first():
            sums = psum.tile([P, 2 * V], F32, name="sums", bufs=2)
            pairs = keep.tile([P, GROUPS, 2, P], F32, name="pairs")
            for g in range(GROUPS):
                gather_words(g)
                squash(0, g)
                y_bank = psum.tile([P, D, P], F32, name="y_bank", bufs=3)
                product_by_feature(y_bank, W1, g)
                sum_y_by_passes(sums[:, V + g * P : V + (g + 1) * P], 0, g)
                ya2 = gate(y_bank, 0, g)
                nc.vector.tensor_tensor(pairs[:, g], ya2[:, 0:2, :], ya2[:, 2:4, :], ALU.add)
            nc.vector.tensor_tensor(
                tables[0][:, :V].rearrange("p (g v) -> p g v", g=GROUPS), pairs[:, :, 0, :], pairs[:, :, 1, :], ALU.add
            )
            other_side(0, sums)

        def encode(t):
            sums = psum.tile([P, 2 * V], F32, name="sums", bufs=2)
            by_passes = t == 1
            for g in range(GROUPS):
                y_bank = psum.tile([P, D, P], F32, name="y_bank", bufs=3)
                product_by_document(y_bank, W1, t, g)
                y_sum = sums[:, V + g * P : V + (g + 1) * P]
                if by_passes:
                    sum_y_by_passes(y_sum, t, g)
                else:
                    y_copy = work.tile([P, D, P], F32, name="y_copy")
                    nc.scalar.copy(y_copy[:], y_bank[:])
                ya2 = gate(y_bank, t, g)
                if not by_passes:
                    sum_by_transposes(y_sum, y_copy)
                sum_by_transposes(sums[:, g * P : (g + 1) * P], ya2)
            nc.scalar.copy(tables[t][:, :V], sums[:, :V])
            other_side(t, sums)

        numer = keep.tile([P, 2, SLOTS, HALF], F32, name="numer")
        inv = keep.tile([P, 2, SLOTS, HALF], F32, name="inv")

        def by_half(values):
            return values.rearrange("p (h r) -> p h r", r=HALF)

        def look_up(t):
            found = work.tile([P, 2, U], F32, name="found")
            nc.vector.tensor_copy(found[:, 0, :], tables[t][:, 0:WINDOW].indirect(doc_t[:]))
            nc.vector.tensor_copy(found[:, 1, :], tables[t][:, V : V + WINDOW].indirect(alt_t[:]))
            return found

        def terms(t, found, cols, tag):
            width = cols.stop - cols.start
            mag = work.tile([P, 2, width], F32, name="mag")
            for side in range(2):
                nc.scalar.activation(mag[:, side, :], found[:, side, cols], ACT.Abs)
            prod = keep.tile([P, 2, width], F32, name="prod", tag=tag)
            for side in range(2):
                nc.vector.scalar_tensor_tensor(
                    prod[:, side, :], found[:, side, cols], unit_t[:, t : t + 1], q_t[side][:, t, cols], ALU.mult, ALU.mult
                )
            return mag, prod

        def invert(target, den, width):
            root = work.tile([P, width], F32, name="root")
            nc.scalar.activation(root[:], den, ACT.Abs_reciprocal_sqrt, bias=two[:])
            nc.scalar.activation(target, by_half(root[:]), ACT.Square)

        def combine(t):
            tag = tanh_tag(LAST, GROUPS - 1) if t == LAST - 1 else "prod%d" % t
            mag, prod = terms(t, look_up(t), slice(0, U), tag)
            nc.gpsimd.tensor_tensor(numer[:, :, t, :], by_half(prod[:, 0, :]), by_half(prod[:, 1, :]), ALU.subtract)
            den = prod[:, 0, :]
            nc.gpsimd.tensor_tensor(den, mag[:, 0, :], mag[:, 1, :], ALU.add)
            invert(inv[:, :, t, :], den, U)

        def combine_last(found, h):
            mag, prod = terms(LAST, found, slice(h * HALF, (h + 1) * HALF), "prod_last%d" % h)
            den = keep.tile([P, HALF], F32, name="den%d" % h)
            nc.vector.tensor_tensor(den[:], mag[:, 0, :], mag[:, 1, :], ALU.add)
            nc.vector.tensor_tensor(numer[:, h : h + 1, LAST, :], by_half(prod[:, 0, :]), by_half(prod[:, 1, :]), ALU.subtract)
            invert(inv[:, h : h + 1, LAST, :], den[:], HALF)

        def project(h):
            hid = work.tile([P, HALF, SLOTS], BF16, name="hid", align_bytes=64)
            nc.vector.tensor_tensor(
                hid[:].rearrange("p (c i) t -> p c t i", i=LINE),
                numer[:, h].rearrange("p t (c i) -> p c t i", i=LINE),
                inv[:, h].rearrange("p t (c i) -> p c t i", i=LINE),
                ALU.mult,
            )
            codes = work.tile([P, HALF], U32, name="codes", align_bytes=64)
            scales = work.tile([P, HALF], U8, name="scales", align_bytes=64)
            nc.vector.quantize_mx(out=codes[:].bitcast(FP8X4), scales=scales[:], in_=flat(hid))
            out_bank = psum.tile([P, HALF], F32, name="out_bank", tag="yb_bank", bufs=3)
            nc.tensor.matmul_mx(
                out=out_bank[:], lhsT=w3w[:].bitcast(FP4X4), lhsT_scale=w3s[:],
                rhs=codes[:].bitcast(FP8X4), rhs_scale=scales[:], start=True, stop=True,
            )
            result = work.tile([P, HALF], F32, name="result")
            nc.scalar.copy(result[:], out_bank[:])
            nc.sync.dma_start(out[:, h * HALF : (h + 1) * HALF], result[:])

        encode_first()
        for t in range(1, SLOTS):
            for g in range(GROUPS):
                squash(t, g)
        for t in range(1, SLOTS):
            encode(t)
        for t in range(LAST):
            combine(t)
        found_last = look_up(LAST)
        for h in range(2):
            combine_last(found_last, h)
        for h in range(2):
            project(h)
